import numpy as np
import ml_dtypes


def mxq(x, axis, fmt="e4m3"):
    dtype, down = {"e4m3": (ml_dtypes.float8_e4m3fn, 7), "e5m2": (ml_dtypes.float8_e5m2, 14)}[fmt]
    v = np.moveaxis(np.asarray(x, np.float32).astype(ml_dtypes.bfloat16).astype(np.float64), axis, -1)
    blocks = v.reshape(v.shape[:-1] + (-1, 32))
    amax = np.abs(blocks).max(-1, keepdims=True)
    byte = np.maximum(np.where(amax > 0, np.frexp(amax)[1] - 1 + 127, 0) - down, 1)
    scale = np.exp2(byte - 127.0)
    codes = (blocks / scale).astype(np.float32).astype(dtype).astype(np.float64)
    return np.moveaxis((codes * scale).reshape(v.shape), -1, axis)


WIDE = False


def mx_kscale(k):
    if not WIDE:
        return np.ones(k)
    levels = np.array([10, -10, 5, -5, 0])
    if k % 512:
        return np.exp2(np.random.permutation(np.resize(levels, k // 32))).repeat(32)
    a = np.empty((k // 512, 16))
    for p in range(k // 512):
        a[p, :8] = np.random.permutation(np.resize(levels, 8))
        for g in range(8):
            far = levels[np.abs(levels - a[p, g]) >= 10]
            a[p, g + 8] = far[np.random.randint(len(far))]
    return np.exp2(a.ravel()).repeat(32)


def f64(x):
    return np.asarray(x).astype(np.float64)


def striped(idx):
    return np.tile(idx.reshape(-1, 16).T, (8, 1)).astype(np.uint16)


def unstriped(offs):
    return offs[:16].T.reshape(-1).astype(np.int64)


E2M1 = np.array([0.0, 0.5, 1.0, 1.5, 2.0, 3.0, 4.0, 6.0, -0.0, -0.5, -1.0, -1.5, -2.0, -3.0, -4.0, -6.0])


def pack_weight(w, fmt):
    k, n = w.shape
    w = f64(np.asarray(w, np.float32).astype(ml_dtypes.bfloat16)).reshape(k // 32, 32, n)
    amax = np.abs(w).max(1)
    if fmt == "e4m3":
        byte = np.frexp(amax)[1] - 1 + 127 - 7
    else:
        mant, ex = np.frexp(amax / 6.0)
        byte = np.where(mant > 0.5, ex, ex - 1) + 127
    byte = np.clip(np.where(amax > 0, byte, 1), 1, 254)
    scaled = (w * np.exp2(127.0 - byte)[:, None, :]).reshape(k, n).astype(np.float32)
    by_word = np.ascontiguousarray(scaled.reshape(k // 512, 128, 4, n).transpose(0, 1, 3, 2))
    if fmt == "e4m3":
        words = by_word.astype(ml_dtypes.float8_e4m3fn).view(np.uint8)
    else:
        c = by_word.astype(ml_dtypes.float4_e2m1fn).view(np.uint8) & 0xF
        words = (c[..., 0::2] | (c[..., 1::2] << 4)).reshape(k // 512, 128, 2 * n)
    return np.ascontiguousarray(words), np.ascontiguousarray(byte.astype(np.uint8).reshape(k // 512, 16, n))


def unpack_weight(words, scales, fmt):
    g, _, n = scales.shape
    words = np.ascontiguousarray(words).reshape(g, 128, n, -1)
    if fmt == "e4m3":
        vals = words.view(ml_dtypes.float8_e4m3fn).astype(np.float64)
    else:
        nib = np.empty((g, 128, n, 4), np.uint8)
        nib[..., 0::2] = words & 0xF
        nib[..., 1::2] = words >> 4
        vals = E2M1[nib]
    vals = vals * np.repeat(np.exp2(scales.astype(np.float64) - 127.0), 8, axis=1)[..., None]
    return vals.transpose(0, 1, 3, 2).reshape(g * 512, n)


def gelu(v):
    return 0.5 * v * (1.0 + np.tanh(np.sqrt(2.0 / np.pi) * (v + 0.044715 * v**3)))


def often(T, S):
    return np.random.permutation(T)[(T * np.random.uniform(0, 1, S) ** 4).astype(np.int64)]


K, K2, T, S, P, H, N = 1024, 512, 2048, 1024, 512, 1024, 256


def setup_inputs():
    n = np.random.standard_normal
    s = mx_kscale(K)[:, None]
    s2 = mx_kscale(K2)[:, None]
    u = mx_kscale(H)[:, None]
    d = {}
    d["tab_words"], d["tab_scales"] = pack_weight(n((K, T)) * s, "e4m3")
    d["tab2_words"], d["tab2_scales"] = pack_weight(n((K2, T)) * s2, "e4m3")
    d["tab3_words"], d["tab3_scales"] = pack_weight(n((K2, T)) * s2, "e4m3")
    d["offs"] = striped(np.random.permutation(T)[:S])
    d["offs2"] = striped(np.random.permutation(T)[:S])
    d["offs3"] = striped(np.random.permutation(T)[:S])
    d["pos1"] = striped(np.random.permutation(S)[:P])
    d["pos2"] = striped(often(S, P))
    d["pos3"] = striped(often(S, P))
    d["wa"] = (n((K, H)) / K ** 0.5 / s * u.T).astype(np.float32)
    d["wb_words"], d["wb_scales"] = pack_weight(1.2 * n((K2, H)) / K2 ** 0.5 / s2, "e2m1")
    d["wd_words"], d["wd_scales"] = pack_weight(n((K2, H)) / K2 ** 0.5 / s2 * u.T, "e4m3")
    d["w4_words"], d["w4_scales"] = pack_weight(1.5 * n((H, N)) / H ** 0.5 / u, "e2m1")
    d["w5"] = (n((H, N)) / H ** 0.5 / u).astype(np.float32)
    d["base"] = (0.7 * n(N)).astype(np.float32)
    return d


def reference(tab_words, tab_scales, tab2_words, tab2_scales, tab3_words, tab3_scales, offs, offs2, offs3, pos1, pos2, pos3, wa, wb_words, wb_scales, wd_words, wd_scales, w4_words, w4_scales, w5, base):
    v = unpack_weight(tab_words, tab_scales, "e4m3")[:, unstriped(offs)]
    v2 = unpack_weight(tab2_words, tab2_scales, "e4m3")[:, unstriped(offs2)]
    v3 = unpack_weight(tab3_words, tab3_scales, "e4m3")[:, unstriped(offs3)]
    a = mxq(f64(wa), 0, "e4m3").T @ v
    b = unpack_weight(wb_words, wb_scales, "e2m1").T @ v2
    d = unpack_weight(wd_words, wd_scales, "e4m3").T @ v3
    z = (a[:, unstriped(pos1)] - d[:, unstriped(pos3)]) / (1.0 + np.square(b[:, unstriped(pos2)]))
    zq = mxq(z, 0, "e4m3")
    size = np.abs(unpack_weight(w4_words, w4_scales, "e2m1").T @ zq)
    side = mxq(f64(w5), 0, "e4m3").T @ zq
    return size + side + f64(base)[:, None]

@@ -1,0 +1,289 @@
+from contextlib import ExitStack
+
+import concourse.mybir as mybir
+
+K, K2, T, S, J, H, N = 1024, 512, 2048, 1024, 512, 1024, 256
+FLOPS = 2 * (K + 2 * K2) * H * S + 2 * 2 * H * N * J
+
+F32 = mybir.dt.float32
+BF16 = mybir.dt.bfloat16
+I32 = mybir.dt.int32
+U32 = mybir.dt.uint32
+U16 = mybir.dt.uint16
+U8 = mybir.dt.uint8
+FP8X4 = mybir.dt.float8_e4m3fn_x4
+FP4X4 = mybir.dt.float4_e2m1fn_x4
+ALU = mybir.AluOpType
+ACT = mybir.ActivationFunctionType
+
+P = 128
+BANK = 512
+
+
+def tile_list_concrete_order_features_kernel(
+    tc, tab_words, tab_scales, tab2_words, tab2_scales, tab3_words, tab3_scales,
+    offs, offs2, offs3, pos1, pos2, pos3, wa, wb_words, wb_scales, wd_words, wd_scales,
+    w4_words, w4_scales, w5, base, out,
+):
+    nc = tc.nc
+    with ExitStack() as ctx:
+        keep = ctx.enter_context(tc.tile_pool(name="keep", bufs=1))
+        ring = ctx.enter_context(tc.tile_pool(name="ring", bufs=2))
+        wins = ctx.enter_context(tc.tile_pool(name="wins", bufs=8))
+        psum = ctx.enter_context(tc.psum_pool(name="psum", bufs=4))
+        psum2 = ctx.enter_context(tc.psum_pool(name="psum2", bufs=1))
+
+        def held(name, shape, dtype, tag=None):
+            return keep.tile(shape, dtype, name=name, tag=tag or name, align_bytes=64)
+
+        def load_list(name, src):
+            t = held(name, list(src.shape), U16)
+            nc.sync.dma_start(t[:], src)
+            return t
+
+        def load_words(name, src, tag=None):
+            t = held(name, [P, src.shape[1]], U32, tag)
+            nc.sync.dma_start(t[:].bitcast(I32), src.rearrange("p n t -> p (n t)").bitcast(I32))
+            return t
+
+        def load_rows(queue, plane, first, scales):
+            rows = 4 * scales.shape[0]
+            for q in range(4):
+                queue.dma_start(
+                    plane[32 * q + first : 32 * q + first + rows, :].bitcast(I32),
+                    (scales[0, 4 * q : 4 * q + 4, :] if rows == 4 else scales[:, 4 * q : 4 * q + 4, :]).bitcast(I32),
+                )
+
+        def load_wa(a, b):
+            t = held("wa_raw%d%d" % (a, b), [P, 4, BANK], F32)
+            nc.sync.dma_start(
+                t[:], wa[512 * a : 512 * (a + 1), 512 * b : 512 * (b + 1)].rearrange("(p j) c -> p j c", j=4)
+            )
+            return t
+
+        sc2 = held("sc2", [P, T], U8)
+        sc3 = held("sc3", [P, T], U8)
+        sc1 = held("sc1", [P, T], U8)
+        wsc_raw = held("wsc_raw", [P, H], U8)
+        w4sc = held("w4sc", [P, 2 * N], U8)
+        nc.gpsimd.memset(sc2[:].bitcast(I32), 0)
+        nc.vector.memset(wsc_raw[:].bitcast(I32), 0)
+        nc.vector.memset(sc3[:].bitcast(I32), 0)
+        nc.vector.memset(sc1[:].bitcast(I32), 0)
+        nc.vector.memset(w4sc[:].bitcast(I32), 0)
+
+        warm = held("warm", [P, 1], F32)
+        warm2 = held("warm2", [P, 1], F32)
+        nc.vector.memset(warm[:], 1.0)
+        nc.scalar.activation(warm2[:], warm[:], ACT.Abs_reciprocal_sqrt)
+
+        wa_raw = {}
+        wb_raw = held("wb_raw", [P, 2 * H], U8)
+        l_offs2 = load_list("l_offs2", offs2)
+        load_rows(nc.sync, sc2, 0, tab2_scales)
+        nc.sync.dma_start(wb_raw[:].bitcast(I32), wb_words[0].bitcast(I32))
+        l_offs3 = load_list("l_offs3", offs3)
+        tw2 = load_words("tw2", tab2_words[0], "slot_tw2")
+        load_rows(nc.sync, wsc_raw, 0, wb_scales)
+        load_rows(nc.sync, wsc_raw, 4, wd_scales)
+        wa_raw[0, 0] = load_wa(0, 0)
+        load_rows(nc.sync, sc3, 4, tab3_scales)
+        tw3 = load_words("tw3", tab3_words[0])
+        l_pos2 = load_list("l_pos2", pos2)
+        wd_raw = load_words("wd_raw", wd_words[0])
+        wa_raw[1, 0] = load_wa(1, 0)
+        l_offs = load_list("l_offs", offs)
+        load_rows(nc.sync, sc1, 8, tab_scales)
+        tw1 = [load_words("tw1%d" % a, tab_words[a]) for a in range(2)]
+        l_pos3 = load_list("l_pos3", pos3)
+        l_pos1 = load_list("l_pos1", pos1)
+        wa_raw[0, 1] = load_wa(0, 1)
+        wa_raw[1, 1] = load_wa(1, 1)
+
+        def gather(name, window, offsets, dtype):
+            t = held(name, [P, S], dtype)
+            nc.vector.tensor_copy(t[:], window[:].indirect(offsets[:]))
+            return t
+
+        def first_stage(passes):
+            win = wins.tile([P, S], F32, name="win")
+            for h in range(2):
+                cols = slice(BANK * h, BANK * (h + 1))
+                acc = psum.tile([P, BANK], F32, name="acc")
+                for i, (w, ws, v, vs) in enumerate(passes):
+                    nc.tensor.matmul_mx(
+                        out=acc[:], lhsT=w, lhsT_scale=ws, rhs=v[:, cols].bitcast(FP8X4), rhs_scale=vs[:, cols],
+                        start=(i == 0), stop=(i == len(passes) - 1),
+                    )
+                nc.scalar.copy(win[:, cols], acc[:])
+            return win
+
+        wb = held("wb", [P, 2 * H], U8)
+        wsc = held("wsc", [P, H], U8)
+        win_b = [wins.tile([P, S], F32, name="win") for u in range(8)]
+        for h in range(2):
+            cols = slice(BANK * h, BANK * (h + 1))
+            entries = l_offs2[:, BANK // 16 * h : BANK // 16 * (h + 1)]
+            gs2 = held("gs2_%d" % h, [P, BANK], U8)
+            gw2 = held("gw2_%d" % h, [P, BANK], U32)
+            nc.vector.tensor_copy(gs2[:], sc2[:].indirect(entries))
+            if h == 0:
+                nc.vector.tensor_copy(
+                    wb[:].bitcast(U16).rearrange("p (b t q) -> p b t q", b=2, t=4),
+                    wb_raw[:].bitcast(U16).rearrange("p (b q t) -> p b t q", b=2, t=4),
+                )
+                nc.vector.tensor_copy(
+                    wsc[:].rearrange("p (b t q) -> p b t q", b=2, t=4),
+                    wsc_raw[:].rearrange("p (b q t) -> p b t q", b=2, t=4),
+                )
+            nc.vector.tensor_copy(gw2[:], tw2[:].indirect(entries))
+            for u in range(8):
+                acc = psum.tile([P, BANK], F32, name="acc")
+                nc.tensor.matmul_mx(
+                    out=acc[:], lhsT=wb[:, 2 * P * u : 2 * P * (u + 1)].bitcast(FP4X4),
+                    lhsT_scale=wsc[:, P * u : P * (u + 1)], rhs=gw2[:].bitcast(FP8X4), rhs_scale=gs2[:],
+                    start=True, stop=True,
+                )
+                nc.scalar.copy(win_b[u][:, cols], acc[:])
+
+        gs3 = gather("gs3", sc3, l_offs3, U8)
+        gw3 = gather("gw3", tw3, l_offs3, U32)
+        wd = held("wd", [P, H], U32)
+        for b in range(2):
+            cols = slice(BANK * b, BANK * (b + 1))
+            nc.vector.tensor_copy(
+                wd[:, cols].bitcast(I32).rearrange("p (t g i) -> p g t i", t=4, i=4),
+                wd_raw[:, cols].bitcast(I32).rearrange("p (g i t) -> p g t i", t=4, i=4),
+            )
+
+        w5_raw = held("w5_raw", [P, 2, 4, N], F32, "slot_tw2")
+        for a in range(2):
+            nc.sync.dma_start(w5_raw[:, a], w5[512 * a : 512 * (a + 1), :].rearrange("(p j) c -> p j c", j=4))
+        w4w = held("w4w", [P, 2, 2 * N], U8)
+        nc.sync.dma_start(w4w[:].bitcast(I32), w4_words.rearrange("a p c -> p a c").bitcast(I32))
+        for q in range(4):
+            nc.sync.dma_start(
+                w4sc[32 * q : 32 * q + 4, :].rearrange("r (a c) -> r a c", a=2).bitcast(I32),
+                w4_scales[:, 4 * q : 4 * q + 4, :].rearrange("a r c -> r a c").bitcast(I32),
+            )
+        base_sb = held("base_sb", [P, 2], F32)
+        with nc.allow_non_contiguous_dma(reason="one value of base a partition"):
+            nc.sync.dma_start(base_sb[:], base.rearrange("(c p) -> p c", p=P))
+
+        picked_b, picked_d, win_d, win_a, damp, diff = {}, {}, {}, {}, {}, {}
+        wa_codes, wa_sc, gw1 = {}, {}, {}
+        acc4 = [psum2.tile([P, J], F32, name="acc4_%d" % c) for c in range(2)]
+        acc5 = [psum2.tile([P, J], F32, name="acc5_%d" % c) for c in range(2)]
+        w5_codes = held("w5_codes", [P, 2 * N], U32)
+        w5_sc = held("w5_sc", [P, 2 * N], U8)
+
+        def pick_b(b):
+            picked_b[b] = ring.tile([P, 4, J], F32, name="picked")
+            for t in range(4):
+                nc.vector.tensor_copy(picked_b[b][:, t, :], win_b[4 * b + t][:].indirect(l_pos2[:]))
+
+        def make_d(b):
+            for u in range(4 * b, 4 * b + 4):
+                win_d[u] = first_stage([(
+                    wd[:, P * u : P * (u + 1)].bitcast(FP8X4), wsc[4:P, P * u : P * (u + 1)], gw3, gs3[4:P, :],
+                )])
+
+        def pick_d(b):
+            picked_d[b] = held("picked_d%d" % b, [P, 4, J], F32)
+            for t in range(4):
+                nc.vector.tensor_copy(picked_d[b][:, t, :], win_d[4 * b + t][:].indirect(l_pos3[:]))
+
+        def quantise_wa(a, b, engine_copy):
+            grouped = ring.tile([P, BANK * 4], BF16, name="grouped", align_bytes=64, bufs=3)
+            engine_copy(
+                grouped[:].rearrange("p (t m j) -> p m t j", t=4, j=4),
+                wa_raw[a, b][:].rearrange("p j (m t) -> p m t j", t=4),
+            )
+            wa_codes[a, b] = held("wa_codes%d%d" % (a, b), [P, BANK], U32)
+            wa_sc[a, b] = held("wa_sc%d%d" % (a, b), [P, BANK], U8)
+            nc.vector.quantize_mx(wa_codes[a, b][:].bitcast(FP8X4), wa_sc[a, b][:], grouped[:])
+
+        def quantise_w5(engine_copy):
+            grouped = ring.tile([P, BANK * 4], BF16, name="grouped", align_bytes=64, bufs=3)
+            for a in range(2):
+                engine_copy(
+                    grouped[:, 4 * N * a : 4 * N * (a + 1)].rearrange("p (c i j) -> p c j i", i=4, j=4),
+                    w5_raw[:, a].rearrange("p j (c i) -> p c j i", i=4),
+                )
+            nc.vector.quantize_mx(w5_codes[:].bitcast(FP8X4), w5_sc[:], grouped[:])
+
+        def make_damp(b):
+            damp[b] = held("damp%d" % b, [P, 4, J], F32)
+            for half in range(2):
+                part = damp[b][:, 2 * half : 2 * half + 2, :]
+                nc.scalar.activation(part, picked_b[b][:, 2 * half : 2 * half + 2, :], ACT.Square)
+                nc.scalar.activation(part, part, ACT.Abs_reciprocal_sqrt, bias=1.0)
+                nc.scalar.activation(part, part, ACT.Square)
+
+        def make_a(b):
+            for t in range(4):
+                cols = slice(P * t, P * (t + 1))
+                win_a[4 * b + t] = first_stage([
+                    (wa_codes[a, b][:, cols].bitcast(FP8X4), wa_sc[a, b][:, cols], gw1[a], gs1[8 + 4 * a : P, :])
+                    for a in range(2)
+                ])
+
+        def pick_a(b):
+            diff[b] = ring.tile([P, 4, J], F32, name="picked")
+            for t in range(4):
+                nc.vector.tensor_tensor(
+                    diff[b][:, t, :], win_a[4 * b + t][:].indirect(l_pos1[:]), picked_d[b][:, t, :], ALU.subtract
+                )
+
+        def second_stage(b):
+            z = ring.tile([P, J * 4], BF16, name="z", align_bytes=64)
+            nc.vector.tensor_tensor(
+                z[:].rearrange("p (c i t) -> p c t i", i=4, t=4),
+                diff[b][:].rearrange("p t (c i) -> p c t i", i=4),
+                damp[b][:].rearrange("p t (c i) -> p c t i", i=4),
+                ALU.mult,
+            )
+            z_codes = ring.tile([P, J], U32, name="z_codes", align_bytes=64)
+            z_sc = ring.tile([P, J], U8, name="z_sc", align_bytes=64)
+            nc.vector.quantize_mx(z_codes[:].bitcast(FP8X4), z_sc[:], z[:])
+            for c in range(2):
+                nc.tensor.matmul_mx(
+                    out=acc4[c][:], lhsT=w4w[:, b, 2 * P * c : 2 * P * (c + 1)].bitcast(FP4X4),
+                    lhsT_scale=w4sc[:, N * b + P * c : N * b + P * (c + 1)],
+                    rhs=z_codes[:].bitcast(FP8X4), rhs_scale=z_sc[:], start=(b == 0), stop=(b == 1),
+                )
+                nc.tensor.matmul_mx(
+                    out=acc5[c][:], lhsT=w5_codes[:, N * b + P * c : N * b + P * (c + 1)].bitcast(FP8X4),
+                    lhsT_scale=w5_sc[:, N * b + P * c : N * b + P * (c + 1)],
+                    rhs=z_codes[:].bitcast(FP8X4), rhs_scale=z_sc[:], start=(b == 0), stop=(b == 1),
+                )
+
+        pick_b(0)
+        pick_b(1)
+        quantise_wa(0, 0, nc.scalar.copy)
+        quantise_wa(1, 0, nc.scalar.copy)
+        gs1 = gather("gs1", sc1, l_offs, U8)
+        for a in range(2):
+            gw1[a] = gather("gw1%d" % a, tw1[a], l_offs, U32)
+        make_d(0)
+        make_d(1)
+        pick_d(0)
+        pick_d(1)
+        quantise_wa(0, 1, nc.scalar.copy)
+        quantise_wa(1, 1, nc.scalar.copy)
+        make_a(0)
+        make_damp(0)
+        pick_a(0)
+        quantise_w5(nc.vector.tensor_copy)
+        second_stage(0)
+        make_a(1)
+        make_damp(1)
+        pick_a(1)
+        second_stage(1)
+
+        for c in range(2):
+            size = ring.tile([P, J], F32, name="size")
+            nc.scalar.activation(size[:], acc4[c][:], ACT.Abs)
+            res = ring.tile([P, J], F32, name="res")
+            nc.vector.scalar_tensor_tensor(res[:], acc5[c][:], base_sb[:, c : c + 1], size[:], ALU.add, ALU.add)
+            nc.sync.dma_start(out[P * c : P * (c + 1), :], res[:])

@@ -18,6 +18,7 @@ ACT = mybir.ActivationFunctionType
 
 P = 128
 BANK = 512
+HALF = 256
 
 
 def tile_list_concrete_order_features_kernel(
@@ -41,25 +42,27 @@ def tile_list_concrete_order_features_kernel(
             nc.sync.dma_start(t[:], src)
             return t
 
-        def load_words(name, src, tag=None):
-            t = held(name, [P, src.shape[1]], U32, tag)
+        def load_words(name, src):
+            t = held(name, [P, src.shape[1]], U32)
             nc.sync.dma_start(t[:].bitcast(I32), src.rearrange("p n t -> p (n t)").bitcast(I32))
             return t
 
-        def load_rows(queue, plane, first, scales):
+        def load_rows(plane, first, scales, quadrants=range(4)):
             rows = 4 * scales.shape[0]
-            for q in range(4):
-                queue.dma_start(
+            for q in quadrants:
+                nc.sync.dma_start(
                     plane[32 * q + first : 32 * q + first + rows, :].bitcast(I32),
                     (scales[0, 4 * q : 4 * q + 4, :] if rows == 4 else scales[:, 4 * q : 4 * q + 4, :]).bitcast(I32),
                 )
 
-        def load_wa(a, b):
-            t = held("wa_raw%d%d" % (a, b), [P, 4, BANK], F32)
+        wa_raw = {}
+
+        def load_wa(a, b, tag=None):
+            wa_raw[a, b] = held("wa_raw%d%d" % (a, b), [P, 4, BANK], F32, tag)
             nc.sync.dma_start(
-                t[:], wa[512 * a : 512 * (a + 1), 512 * b : 512 * (b + 1)].rearrange("(p j) c -> p j c", j=4)
+                wa_raw[a, b][:],
+                wa[512 * a : 512 * (a + 1), 512 * b : 512 * (b + 1)].rearrange("(p j) c -> p j c", j=4),
             )
-            return t
 
         sc2 = held("sc2", [P, T], U8)
         sc3 = held("sc3", [P, T], U8)
@@ -77,56 +80,56 @@ def tile_list_concrete_order_features_kernel(
         nc.vector.memset(warm[:], 1.0)
         nc.scalar.activation(warm2[:], warm[:], ACT.Abs_reciprocal_sqrt)
 
-        wa_raw = {}
         wb_raw = held("wb_raw", [P, 2 * H], U8)
         l_offs2 = load_list("l_offs2", offs2)
-        load_rows(nc.sync, sc2, 0, tab2_scales)
+        load_rows(sc2, 0, tab2_scales)
         nc.sync.dma_start(wb_raw[:].bitcast(I32), wb_words[0].bitcast(I32))
+        load_rows(wsc_raw, 0, wb_scales, range(1))
+        tw2 = load_words("tw2", tab2_words[0])
+        load_rows(wsc_raw, 0, wb_scales, range(1, 4))
+        load_rows(wsc_raw, 4, wd_scales)
         l_offs3 = load_list("l_offs3", offs3)
-        tw2 = load_words("tw2", tab2_words[0], "slot_tw2")
-        load_rows(nc.sync, wsc_raw, 0, wb_scales)
-        load_rows(nc.sync, wsc_raw, 4, wd_scales)
-        wa_raw[0, 0] = load_wa(0, 0)
-        load_rows(nc.sync, sc3, 4, tab3_scales)
+        load_rows(sc3, 4, tab3_scales)
         tw3 = load_words("tw3", tab3_words[0])
-        l_pos2 = load_list("l_pos2", pos2)
         wd_raw = load_words("wd_raw", wd_words[0])
-        wa_raw[1, 0] = load_wa(1, 0)
         l_offs = load_list("l_offs", offs)
-        load_rows(nc.sync, sc1, 8, tab_scales)
-        tw1 = [load_words("tw1%d" % a, tab_words[a]) for a in range(2)]
+        load_rows(sc1, 8, tab_scales)
+        l_pos2 = load_list("l_pos2", pos2)
+        load_wa(0, 0)
+        load_wa(1, 0)
+        tw10 = load_words("tw10", tab_words[0])
+        tw11 = load_words("tw11", tab_words[1])
         l_pos3 = load_list("l_pos3", pos3)
         l_pos1 = load_list("l_pos1", pos1)
-        wa_raw[0, 1] = load_wa(0, 1)
-        wa_raw[1, 1] = load_wa(1, 1)
 
         def gather(name, window, offsets, dtype):
-            t = held(name, [P, S], dtype)
-            nc.vector.tensor_copy(t[:], window[:].indirect(offsets[:]))
+            t = held(name, [P, 16 * offsets.shape[1]], dtype)
+            nc.vector.tensor_copy(t[:], window[:].indirect(offsets))
             return t
 
-        def first_stage(passes):
-            win = wins.tile([P, S], F32, name="win")
-            for h in range(2):
-                cols = slice(BANK * h, BANK * (h + 1))
-                acc = psum.tile([P, BANK], F32, name="acc")
-                for i, (w, ws, v, vs) in enumerate(passes):
-                    nc.tensor.matmul_mx(
-                        out=acc[:], lhsT=w, lhsT_scale=ws, rhs=v[:, cols].bitcast(FP8X4), rhs_scale=vs[:, cols],
-                        start=(i == 0), stop=(i == len(passes) - 1),
-                    )
-                nc.scalar.copy(win[:, cols], acc[:])
-            return win
+        def product(win, h, passes):
+            cols = slice(BANK * h, BANK * (h + 1))
+            acc = psum.tile([P, BANK], F32, name="acc")
+            for i, (w, ws, v, vs) in enumerate(passes):
+                nc.tensor.matmul_mx(
+                    out=acc[:], lhsT=w, lhsT_scale=ws, rhs=v.bitcast(FP8X4), rhs_scale=vs,
+                    start=(i == 0), stop=(i == len(passes) - 1),
+                )
+            nc.scalar.copy(win[:, cols], acc[:])
+
+        def halves(ap):
+            return [ap[:, BANK * h : BANK * (h + 1)] for h in range(2)]
+
+        win_b, win_d, win_a = {}, {}, {}
+        picked_b, picked_d, picked_a, damp = {}, {}, {}, {}
+        wa_codes, wa_sc = {}, {}
 
         wb = held("wb", [P, 2 * H], U8)
         wsc = held("wsc", [P, H], U8)
-        win_b = [wins.tile([P, S], F32, name="win") for u in range(8)]
+        gs2, gw2 = [], []
         for h in range(2):
-            cols = slice(BANK * h, BANK * (h + 1))
             entries = l_offs2[:, BANK // 16 * h : BANK // 16 * (h + 1)]
-            gs2 = held("gs2_%d" % h, [P, BANK], U8)
-            gw2 = held("gw2_%d" % h, [P, BANK], U32)
-            nc.vector.tensor_copy(gs2[:], sc2[:].indirect(entries))
+            gs2.append(gather("gs2_%d" % h, sc2, entries, U8))
             if h == 0:
                 nc.vector.tensor_copy(
                     wb[:].bitcast(U16).rearrange("p (b t q) -> p b t q", b=2, t=4),
@@ -136,18 +139,21 @@ def tile_list_concrete_order_features_kernel(
                     wsc[:].rearrange("p (b t q) -> p b t q", b=2, t=4),
                     wsc_raw[:].rearrange("p (b q t) -> p b t q", b=2, t=4),
                 )
-            nc.vector.tensor_copy(gw2[:], tw2[:].indirect(entries))
-            for u in range(8):
-                acc = psum.tile([P, BANK], F32, name="acc")
-                nc.tensor.matmul_mx(
-                    out=acc[:], lhsT=wb[:, 2 * P * u : 2 * P * (u + 1)].bitcast(FP4X4),
-                    lhsT_scale=wsc[:, P * u : P * (u + 1)], rhs=gw2[:].bitcast(FP8X4), rhs_scale=gs2[:],
-                    start=True, stop=True,
-                )
-                nc.scalar.copy(win_b[u][:, cols], acc[:])
+            gw2.append(gather("gw2_%d" % h, tw2, entries, U32))
 
-        gs3 = gather("gs3", sc3, l_offs3, U8)
-        gw3 = gather("gw3", tw3, l_offs3, U32)
+        def make_b(b):
+            for u in range(4 * b, 4 * b + 4):
+                win_b[u] = wins.tile([P, S], F32, name="win")
+            for h in range(2):
+                for u in range(4 * b, 4 * b + 4):
+                    product(win_b[u], h, [(
+                        wb[:, 2 * P * u : 2 * P * (u + 1)].bitcast(FP4X4), wsc[:, P * u : P * (u + 1)],
+                        gw2[h][:], gs2[h][:],
+                    )])
+
+        make_b(0)
+        gs3 = gather("gs3", sc3, l_offs3[:], U8)
+        gw3 = gather("gw3", tw3, l_offs3[:], U32)
         wd = held("wd", [P, H], U32)
         for b in range(2):
             cols = slice(BANK * b, BANK * (b + 1))
@@ -156,9 +162,8 @@ def tile_list_concrete_order_features_kernel(
                 wd_raw[:, cols].bitcast(I32).rearrange("p (g i t) -> p g t i", t=4, i=4),
             )
 
-        w5_raw = held("w5_raw", [P, 2, 4, N], F32, "slot_tw2")
-        for a in range(2):
-            nc.sync.dma_start(w5_raw[:, a], w5[512 * a : 512 * (a + 1), :].rearrange("(p j) c -> p j c", j=4))
+        load_wa(0, 1, "tw2")
+        load_wa(1, 1, "tw3")
         w4w = held("w4w", [P, 2, 2 * N], U8)
         nc.sync.dma_start(w4w[:].bitcast(I32), w4_words.rearrange("a p c -> p a c").bitcast(I32))
         for q in range(4):
@@ -170,42 +175,50 @@ def tile_list_concrete_order_features_kernel(
         with nc.allow_non_contiguous_dma(reason="one value of base a partition"):
             nc.sync.dma_start(base_sb[:], base.rearrange("(c p) -> p c", p=P))
 
-        picked_b, picked_d, win_d, win_a, damp, diff = {}, {}, {}, {}, {}, {}
-        wa_codes, wa_sc, gw1 = {}, {}, {}
-        acc4 = [psum2.tile([P, J], F32, name="acc4_%d" % c) for c in range(2)]
-        acc5 = [psum2.tile([P, J], F32, name="acc5_%d" % c) for c in range(2)]
+        acc4 = [psum2.tile([P, BANK], F32, name="acc4_%d" % h) for h in range(2)]
+        acc5 = [psum2.tile([P, BANK], F32, name="acc5_%d" % h) for h in range(2)]
         w5_codes = held("w5_codes", [P, 2 * N], U32)
         w5_sc = held("w5_sc", [P, 2 * N], U8)
 
-        def pick_b(b):
-            picked_b[b] = ring.tile([P, 4, J], F32, name="picked")
+        def pick(wins_of, b, entries, into):
             for t in range(4):
-                nc.vector.tensor_copy(picked_b[b][:, t, :], win_b[4 * b + t][:].indirect(l_pos2[:]))
+                nc.vector.tensor_copy(into[:, t, :], wins_of[4 * b + t][:].indirect(entries[:]))
 
-        def make_d(b):
-            for u in range(4 * b, 4 * b + 4):
-                win_d[u] = first_stage([(
-                    wd[:, P * u : P * (u + 1)].bitcast(FP8X4), wsc[4:P, P * u : P * (u + 1)], gw3, gs3[4:P, :],
-                )])
+        def pick_b(b):
+            picked_b[b] = ring.tile([P, 4, J], F32, name="picked", bufs=3)
+            pick(win_b, b, l_pos2, picked_b[b])
 
         def pick_d(b):
             picked_d[b] = held("picked_d%d" % b, [P, 4, J], F32)
-            for t in range(4):
-                nc.vector.tensor_copy(picked_d[b][:, t, :], win_d[4 * b + t][:].indirect(l_pos3[:]))
+            pick(win_d, b, l_pos3, picked_d[b])
 
-        def quantise_wa(a, b, engine_copy):
-            grouped = ring.tile([P, BANK * 4], BF16, name="grouped", align_bytes=64, bufs=3)
-            engine_copy(
-                grouped[:].rearrange("p (t m j) -> p m t j", t=4, j=4),
-                wa_raw[a, b][:].rearrange("p j (m t) -> p m t j", t=4),
-            )
+        def make_d(b):
+            for u in range(4 * b, 4 * b + 4):
+                win_d[u] = wins.tile([P, S], F32, name="win")
+                for h in range(2):
+                    product(win_d[u], h, [(
+                        wd[:, P * u : P * (u + 1)].bitcast(FP8X4), wsc[4:P, P * u : P * (u + 1)],
+                        halves(gw3)[h], halves(gs3[4:P, :])[h],
+                    )])
+
+        def gpsimd_copy(dst, src):
+            nc.gpsimd.tensor_scalar(dst, src, 1.0, 0.0, ALU.mult, ALU.add)
+
+        def quantise_wa(a, b):
+            grouped = ring.tile([P, BANK * 4], BF16, name="grouped", align_bytes=64, bufs=4)
+            dst = grouped[:].rearrange("p (t m j) -> p m t j", t=4, j=4)
+            src = wa_raw[a, b][:].rearrange("p j (m t) -> p m t j", t=4)
+            for m0 in range(0, P, 32):
+                gpsimd_copy(dst[:, m0 : m0 + 32], src[:, m0 : m0 + 32])
             wa_codes[a, b] = held("wa_codes%d%d" % (a, b), [P, BANK], U32)
             wa_sc[a, b] = held("wa_sc%d%d" % (a, b), [P, BANK], U8)
             nc.vector.quantize_mx(wa_codes[a, b][:].bitcast(FP8X4), wa_sc[a, b][:], grouped[:])
 
         def quantise_w5(engine_copy):
-            grouped = ring.tile([P, BANK * 4], BF16, name="grouped", align_bytes=64, bufs=3)
+            w5_raw = held("w5_raw", [P, 2, 4, N], F32, "wa_raw00")
+            grouped = ring.tile([P, BANK * 4], BF16, name="grouped", align_bytes=64, bufs=4)
             for a in range(2):
+                nc.sync.dma_start(w5_raw[:, a], w5[512 * a : 512 * (a + 1), :].rearrange("(p j) c -> p j c", j=4))
                 engine_copy(
                     grouped[:, 4 * N * a : 4 * N * (a + 1)].rearrange("p (c i j) -> p c j i", i=4, j=4),
                     w5_raw[:, a].rearrange("p j (c i) -> p c j i", i=4),
@@ -223,67 +236,89 @@ def tile_list_concrete_order_features_kernel(
         def make_a(b):
             for t in range(4):
                 cols = slice(P * t, P * (t + 1))
-                win_a[4 * b + t] = first_stage([
-                    (wa_codes[a, b][:, cols].bitcast(FP8X4), wa_sc[a, b][:, cols], gw1[a], gs1[8 + 4 * a : P, :])
-                    for a in range(2)
-                ])
+                win_a[4 * b + t] = wins.tile([P, S], F32, name="win")
+                for h in range(2):
+                    product(win_a[4 * b + t], h, [
+                        (wa_codes[a, b][:, cols].bitcast(FP8X4), wa_sc[a, b][:, cols],
+                         halves(gw1[a])[h], halves(gs1[8 + 4 * a : P, :])[h])
+                        for a in range(2)
+                    ])
 
-        def pick_a(b):
-            diff[b] = ring.tile([P, 4, J], F32, name="picked")
+        def pick_a(b, engines):
+            picked_a[b] = ring.tile([P, 4, J], F32, name="picked", bufs=3)
+            pick(win_a, b, l_pos1, picked_a[b])
             for t in range(4):
-                nc.vector.tensor_tensor(
-                    diff[b][:, t, :], win_a[4 * b + t][:].indirect(l_pos1[:]), picked_d[b][:, t, :], ALU.subtract
+                engines[t].tensor_tensor(
+                    picked_d[b][:, t, :], picked_a[b][:, t, :], picked_d[b][:, t, :], ALU.subtract
                 )
 
-        def second_stage(b):
-            z = ring.tile([P, J * 4], BF16, name="z", align_bytes=64)
-            nc.vector.tensor_tensor(
-                z[:].rearrange("p (c i t) -> p c t i", i=4, t=4),
-                diff[b][:].rearrange("p t (c i) -> p c t i", i=4),
-                damp[b][:].rearrange("p t (c i) -> p c t i", i=4),
-                ALU.mult,
-            )
+        def second_stage(b, engine, width, run):
             z_codes = ring.tile([P, J], U32, name="z_codes", align_bytes=64)
             z_sc = ring.tile([P, J], U8, name="z_sc", align_bytes=64)
-            nc.vector.quantize_mx(z_codes[:].bitcast(FP8X4), z_sc[:], z[:])
-            for c in range(2):
-                nc.tensor.matmul_mx(
-                    out=acc4[c][:], lhsT=w4w[:, b, 2 * P * c : 2 * P * (c + 1)].bitcast(FP4X4),
-                    lhsT_scale=w4sc[:, N * b + P * c : N * b + P * (c + 1)],
-                    rhs=z_codes[:].bitcast(FP8X4), rhs_scale=z_sc[:], start=(b == 0), stop=(b == 1),
+            for j0 in range(0, J, width):
+                if j0 % run == 0:
+                    z = held("z%d_%d" % (b, j0), [P, run * 4], BF16, "z%d" % b)
+                at = j0 % run
+                engine.tensor_tensor(
+                    z[:, 4 * at : 4 * (at + width)].rearrange("p (c i t) -> p c t i", i=4, t=4),
+                    picked_d[b][:, :, j0 : j0 + width].rearrange("p t (c i) -> p c t i", i=4),
+                    damp[b][:, :, j0 : j0 + width].rearrange("p t (c i) -> p c t i", i=4),
+                    ALU.mult,
                 )
-                nc.tensor.matmul_mx(
-                    out=acc5[c][:], lhsT=w5_codes[:, N * b + P * c : N * b + P * (c + 1)].bitcast(FP8X4),
-                    lhsT_scale=w5_sc[:, N * b + P * c : N * b + P * (c + 1)],
-                    rhs=z_codes[:].bitcast(FP8X4), rhs_scale=z_sc[:], start=(b == 0), stop=(b == 1),
-                )
+                j1 = j0 + width
+                if j1 % run == 0:
+                    nc.vector.quantize_mx(
+                        z_codes[:, j1 - run : j1].bitcast(FP8X4), z_sc[:, j1 - run : j1], z[:]
+                    )
+            for h in range(2):
+                for c in range(2):
+                    wcols = slice(N * b + P * c, N * b + P * (c + 1))
+                    for y in range(2):
+                        zc = slice(HALF * h + P * y, HALF * h + P * (y + 1))
+                        nc.tensor.matmul_mx(
+                            out=acc4[h][:, HALF * c + P * y : HALF * c + P * (y + 1)],
+                            lhsT=w4w[:, b, 2 * P * c : 2 * P * (c + 1)].bitcast(FP4X4),
+                            lhsT_scale=w4sc[:, wcols], rhs=z_codes[:, zc].bitcast(FP8X4), rhs_scale=z_sc[:, zc],
+                            start=(b == 0 and c == 0 and y == 0), stop=(b == 1 and c == 1 and y == 1),
+                        )
+                zc = slice(HALF * h, HALF * (h + 1))
+                for c in range(2):
+                    wcols = slice(N * b + P * c, N * b + P * (c + 1))
+                    nc.tensor.matmul_mx(
+                        out=acc5[h][:, HALF * c : HALF * (c + 1)], lhsT=w5_codes[:, wcols].bitcast(FP8X4),
+                        lhsT_scale=w5_sc[:, wcols], rhs=z_codes[:, zc].bitcast(FP8X4), rhs_scale=z_sc[:, zc],
+                        start=(b == 0 and c == 0), stop=(b == 1 and c == 1),
+                    )
+                if b == 1:
+                    size = ring.tile([P, BANK], F32, name="size")
+                    res = ring.tile([P, 2, HALF], F32, name="res")
+                    for c in range(2):
+                        cols = slice(HALF * c, HALF * (c + 1))
+                        nc.scalar.activation(size[:, cols], acc4[h][:, cols], ACT.Abs)
+                        nc.vector.scalar_tensor_tensor(
+                            res[:, c, :], acc5[h][:, cols], base_sb[:, c : c + 1], size[:, cols], ALU.add, ALU.add
+                        )
+                        nc.sync.dma_start(out[P * c : P * (c + 1), HALF * h : HALF * (h + 1)], res[:, c, :])
 
         pick_b(0)
-        pick_b(1)
-        quantise_wa(0, 0, nc.scalar.copy)
-        quantise_wa(1, 0, nc.scalar.copy)
-        gs1 = gather("gs1", sc1, l_offs, U8)
-        for a in range(2):
-            gw1[a] = gather("gw1%d" % a, tw1[a], l_offs, U32)
         make_d(0)
-        make_d(1)
-        pick_d(0)
-        pick_d(1)
-        quantise_wa(0, 1, nc.scalar.copy)
-        quantise_wa(1, 1, nc.scalar.copy)
-        make_a(0)
+        quantise_wa(0, 0)
+        quantise_wa(1, 0)
+        gs1 = gather("gs1", sc1, l_offs[:], U8)
+        gw1 = [gather("gw10", tw10, l_offs[:], U32), gather("gw11", tw11, l_offs[:], U32)]
         make_damp(0)
-        pick_a(0)
-        quantise_w5(nc.vector.tensor_copy)
-        second_stage(0)
+        quantise_wa(0, 1)
+        quantise_wa(1, 1)
+        quantise_w5(gpsimd_copy)
+        make_a(0)
+        make_b(1)
+        pick_d(0)
+        pick_a(0, [nc.gpsimd, nc.gpsimd, nc.gpsimd, nc.gpsimd])
+        pick_b(1)
+        make_d(1)
+        second_stage(0, nc.gpsimd, 128, J)
+        pick_d(1)
         make_a(1)
         make_damp(1)
-        pick_a(1)
-        second_stage(1)
-
-        for c in range(2):
-            size = ring.tile([P, J], F32, name="size")
-            nc.scalar.activation(size[:], acc4[c][:], ACT.Abs)
-            res = ring.tile([P, J], F32, name="res")
-            nc.vector.scalar_tensor_tensor(res[:], acc5[c][:], base_sb[:, c : c + 1], size[:], ALU.add, ALU.add)
-            nc.sync.dma_start(out[P * c : P * (c + 1), :], res[:])
+        pick_a(1, [nc.gpsimd, nc.gpsimd, nc.gpsimd, nc.vector])
+        second_stage(1, nc.vector, 256, 256)

@@ -30,12 +30,16 @@ def tile_list_concrete_order_features_kernel(
     with ExitStack() as ctx:
         keep = ctx.enter_context(tc.tile_pool(name="keep", bufs=1))
         ring = ctx.enter_context(tc.tile_pool(name="ring", bufs=2))
-        wins = ctx.enter_context(tc.tile_pool(name="wins", bufs=8))
-        psum = ctx.enter_context(tc.psum_pool(name="psum", bufs=4))
-        psum2 = ctx.enter_context(tc.psum_pool(name="psum2", bufs=1))
+        psum = ctx.enter_context(tc.psum_pool(name="psum", bufs=1))
 
         def held(name, shape, dtype, tag=None):
             return keep.tile(shape, dtype, name=name, tag=tag or name, align_bytes=64)
+
+        banks = []
+
+        def next_bank():
+            banks.append(psum.tile([P, BANK], F32, name="bank%d" % (len(banks) % 8)))
+            return banks[-1]
 
         def load_list(name, src):
             t = held(name, list(src.shape), U16)
@@ -109,7 +113,7 @@ def tile_list_concrete_order_features_kernel(
 
         def product(win, h, passes):
             cols = slice(BANK * h, BANK * (h + 1))
-            acc = psum.tile([P, BANK], F32, name="acc")
+            acc = next_bank()
             for i, (w, ws, v, vs) in enumerate(passes):
                 nc.tensor.matmul_mx(
                     out=acc[:], lhsT=w, lhsT_scale=ws, rhs=v.bitcast(FP8X4), rhs_scale=vs,
@@ -121,7 +125,7 @@ def tile_list_concrete_order_features_kernel(
             return [ap[:, BANK * h : BANK * (h + 1)] for h in range(2)]
 
         win_b, win_d, win_a = {}, {}, {}
-        picked_b, picked_d, picked_a, damp = {}, {}, {}, {}
+        picked_b, picked_d, diff, damp = {}, {}, {}, {}
         wa_codes, wa_sc = {}, {}
 
         wb = held("wb", [P, 2 * H], U8)
@@ -143,7 +147,7 @@ def tile_list_concrete_order_features_kernel(
 
         def make_b(b):
             for u in range(4 * b, 4 * b + 4):
-                win_b[u] = wins.tile([P, S], F32, name="win")
+                win_b[u] = held("win_b%d" % u, [P, S], F32, "win%d" % (u + 4 * b))
             for h in range(2):
                 for u in range(4 * b, 4 * b + 4):
                     product(win_b[u], h, [(
@@ -162,6 +166,9 @@ def tile_list_concrete_order_features_kernel(
                 wd_raw[:, cols].bitcast(I32).rearrange("p (g i t) -> p g t i", t=4, i=4),
             )
 
+        w5_raw = held("w5_raw", [P, 2, 4, N], F32)
+        for a in range(2):
+            nc.sync.dma_start(w5_raw[:, a], w5[512 * a : 512 * (a + 1), :].rearrange("(p j) c -> p j c", j=4))
         load_wa(0, 1, "tw2")
         load_wa(1, 1, "tw3")
         w4w = held("w4w", [P, 2, 2 * N], U8)
@@ -175,8 +182,7 @@ def tile_list_concrete_order_features_kernel(
         with nc.allow_non_contiguous_dma(reason="one value of base a partition"):
             nc.sync.dma_start(base_sb[:], base.rearrange("(c p) -> p c", p=P))
 
-        acc4 = [psum2.tile([P, BANK], F32, name="acc4_%d" % h) for h in range(2)]
-        acc5 = [psum2.tile([P, BANK], F32, name="acc5_%d" % h) for h in range(2)]
+        acc4, acc5, zq = {}, {}, {}
         w5_codes = held("w5_codes", [P, 2 * N], U32)
         w5_sc = held("w5_sc", [P, 2 * N], U8)
 
@@ -185,7 +191,10 @@ def tile_list_concrete_order_features_kernel(
                 nc.vector.tensor_copy(into[:, t, :], wins_of[4 * b + t][:].indirect(entries[:]))
 
         def pick_b(b):
-            picked_b[b] = ring.tile([P, 4, J], F32, name="picked", bufs=3)
+            if b == 0:
+                picked_b[b] = held("picked_b0", [P, 4, J], F32)
+            else:
+                picked_b[b] = held("picked_b1", [P, 4, J], F32, "picked_d0")
             pick(win_b, b, l_pos2, picked_b[b])
 
         def pick_d(b):
@@ -194,7 +203,7 @@ def tile_list_concrete_order_features_kernel(
 
         def make_d(b):
             for u in range(4 * b, 4 * b + 4):
-                win_d[u] = wins.tile([P, S], F32, name="win")
+                win_d[u] = held("win_d%d" % u, [P, S], F32, "win%d" % ((4 + u) % 8))
                 for h in range(2):
                     product(win_d[u], h, [(
                         wd[:, P * u : P * (u + 1)].bitcast(FP8X4), wsc[4:P, P * u : P * (u + 1)],
@@ -205,23 +214,21 @@ def tile_list_concrete_order_features_kernel(
             nc.gpsimd.tensor_scalar(dst, src, 1.0, 0.0, ALU.mult, ALU.add)
 
         def quantise_wa(a, b):
-            grouped = ring.tile([P, BANK * 4], BF16, name="grouped", align_bytes=64, bufs=4)
+            grouped = held("grouped%d%d" % (a, b), [P, BANK * 4], BF16, "grouped%d" % a)
             dst = grouped[:].rearrange("p (t m j) -> p m t j", t=4, j=4)
             src = wa_raw[a, b][:].rearrange("p j (m t) -> p m t j", t=4)
-            for m0 in range(0, P, 32):
-                gpsimd_copy(dst[:, m0 : m0 + 32], src[:, m0 : m0 + 32])
+            for m0 in range(0, P, 64):
+                gpsimd_copy(dst[:, m0 : m0 + 64], src[:, m0 : m0 + 64])
             wa_codes[a, b] = held("wa_codes%d%d" % (a, b), [P, BANK], U32)
             wa_sc[a, b] = held("wa_sc%d%d" % (a, b), [P, BANK], U8)
             nc.vector.quantize_mx(wa_codes[a, b][:].bitcast(FP8X4), wa_sc[a, b][:], grouped[:])
 
         def quantise_w5(engine_copy):
-            w5_raw = held("w5_raw", [P, 2, 4, N], F32, "wa_raw00")
-            grouped = ring.tile([P, BANK * 4], BF16, name="grouped", align_bytes=64, bufs=4)
+            grouped = held("grouped_w5", [P, BANK * 4], BF16)
             for a in range(2):
-                nc.sync.dma_start(w5_raw[:, a], w5[512 * a : 512 * (a + 1), :].rearrange("(p j) c -> p j c", j=4))
                 engine_copy(
-                    grouped[:, 4 * N * a : 4 * N * (a + 1)].rearrange("p (c i j) -> p c j i", i=4, j=4),
-                    w5_raw[:, a].rearrange("p j (c i) -> p c j i", i=4),
+                    grouped[:, 4 * N * a : 4 * N * (a + 1)].rearrange("p (c j) -> p c j", j=4),
+                    w5_raw[:, a].rearrange("p j c -> p c j"),
                 )
             nc.vector.quantize_mx(w5_codes[:].bitcast(FP8X4), w5_sc[:], grouped[:])
 
@@ -236,7 +243,7 @@ def tile_list_concrete_order_features_kernel(
         def make_a(b):
             for t in range(4):
                 cols = slice(P * t, P * (t + 1))
-                win_a[4 * b + t] = wins.tile([P, S], F32, name="win")
+                win_a[4 * b + t] = held("win_a%d" % (4 * b + t), [P, S], F32, "win%d" % (4 * b + t))
                 for h in range(2):
                     product(win_a[4 * b + t], h, [
                         (wa_codes[a, b][:, cols].bitcast(FP8X4), wa_sc[a, b][:, cols],
@@ -244,12 +251,11 @@ def tile_list_concrete_order_features_kernel(
                         for a in range(2)
                     ])
 
-        def pick_a(b, engines):
-            picked_a[b] = ring.tile([P, 4, J], F32, name="picked", bufs=3)
-            pick(win_a, b, l_pos1, picked_a[b])
+        def pick_a(b):
+            diff[b] = held("diff%d" % b, [P, 4, J], F32, ("grouped1", "picked_b0")[b])
             for t in range(4):
-                engines[t].tensor_tensor(
-                    picked_d[b][:, t, :], picked_a[b][:, t, :], picked_d[b][:, t, :], ALU.subtract
+                nc.vector.tensor_tensor(
+                    diff[b][:, t, :], win_a[4 * b + t][:].indirect(l_pos1[:]), picked_d[b][:, t, :], ALU.subtract
                 )
 
         def second_stage(b, engine, width, run):
@@ -261,7 +267,7 @@ def tile_list_concrete_order_features_kernel(
                 at = j0 % run
                 engine.tensor_tensor(
                     z[:, 4 * at : 4 * (at + width)].rearrange("p (c i t) -> p c t i", i=4, t=4),
-                    picked_d[b][:, :, j0 : j0 + width].rearrange("p t (c i) -> p c t i", i=4),
+                    diff[b][:, :, j0 : j0 + width].rearrange("p t (c i) -> p c t i", i=4),
                     damp[b][:, :, j0 : j0 + width].rearrange("p t (c i) -> p c t i", i=4),
                     ALU.mult,
                 )
@@ -270,7 +276,14 @@ def tile_list_concrete_order_features_kernel(
                     nc.vector.quantize_mx(
                         z_codes[:, j1 - run : j1].bitcast(FP8X4), z_sc[:, j1 - run : j1], z[:]
                     )
+            zq[b] = z_codes, z_sc
+
+        def multiply_z(b):
+            z_codes, z_sc = zq[b]
             for h in range(2):
+                if b == 0:
+                    acc4[h] = next_bank()
+                    acc5[h] = next_bank()
                 for c in range(2):
                     wcols = slice(N * b + P * c, N * b + P * (c + 1))
                     for y in range(2):
@@ -307,18 +320,20 @@ def tile_list_concrete_order_features_kernel(
         gs1 = gather("gs1", sc1, l_offs[:], U8)
         gw1 = [gather("gw10", tw10, l_offs[:], U32), gather("gw11", tw11, l_offs[:], U32)]
         make_damp(0)
+        quantise_w5(gpsimd_copy)
         quantise_wa(0, 1)
         quantise_wa(1, 1)
-        quantise_w5(gpsimd_copy)
-        make_a(0)
         make_b(1)
+        make_a(0)
         pick_d(0)
-        pick_a(0, [nc.gpsimd, nc.gpsimd, nc.gpsimd, nc.gpsimd])
+        pick_a(0)
         pick_b(1)
         make_d(1)
-        second_stage(0, nc.gpsimd, 128, J)
+        second_stage(0, nc.gpsimd, 64, J)
         pick_d(1)
         make_a(1)
+        multiply_z(0)
         make_damp(1)
-        pick_a(1, [nc.gpsimd, nc.gpsimd, nc.gpsimd, nc.vector])
+        pick_a(1)
         second_stage(1, nc.vector, 256, 256)
+        multiply_z(1)

from contextlib import ExitStack

import concourse.mybir as mybir

K, K2, T, S, J, H, N = 1024, 512, 2048, 1024, 512, 1024, 256
FLOPS = 2 * (K + 2 * K2) * H * S + 2 * 2 * H * N * J

F32 = mybir.dt.float32
BF16 = mybir.dt.bfloat16
I32 = mybir.dt.int32
U32 = mybir.dt.uint32
U16 = mybir.dt.uint16
U8 = mybir.dt.uint8
FP8X4 = mybir.dt.float8_e4m3fn_x4
FP4X4 = mybir.dt.float4_e2m1fn_x4
ALU = mybir.AluOpType
ACT = mybir.ActivationFunctionType

P = 128
BANK = 512
HALF = 256


def tile_list_concrete_order_features_kernel(
    tc, tab_words, tab_scales, tab2_words, tab2_scales, tab3_words, tab3_scales,
    offs, offs2, offs3, pos1, pos2, pos3, wa, wb_words, wb_scales, wd_words, wd_scales,
    w4_words, w4_scales, w5, base, out,
):
    nc = tc.nc
    with ExitStack() as ctx:
        keep = ctx.enter_context(tc.tile_pool(name="keep", bufs=1))
        ring = ctx.enter_context(tc.tile_pool(name="ring", bufs=2))
        psum = ctx.enter_context(tc.psum_pool(name="psum", bufs=1))

        def held(name, shape, dtype, tag=None):
            return keep.tile(shape, dtype, name=name, tag=tag or name, align_bytes=64)

        banks = []

        def next_bank():
            banks.append(psum.tile([P, BANK], F32, name="bank%d" % (len(banks) % 8)))
            return banks[-1]

        def load_list(name, src):
            t = held(name, list(src.shape), U16)
            nc.sync.dma_start(t[:], src)
            return t

        def load_words(name, src):
            t = held(name, [P, src.shape[1]], U32)
            nc.sync.dma_start(t[:].bitcast(I32), src.rearrange("p n t -> p (n t)").bitcast(I32))
            return t

        def load_rows(plane, first, scales, quadrants=range(4)):
            rows = 4 * scales.shape[0]
            for q in quadrants:
                nc.sync.dma_start(
                    plane[32 * q + first : 32 * q + first + rows, :].bitcast(I32),
                    (scales[0, 4 * q : 4 * q + 4, :] if rows == 4 else scales[:, 4 * q : 4 * q + 4, :]).bitcast(I32),
                )

        wa_raw = {}

        def load_wa(a, b, tag=None):
            wa_raw[a, b] = held("wa_raw%d%d" % (a, b), [P, 4, BANK], F32, tag)
            nc.sync.dma_start(
                wa_raw[a, b][:],
                wa[512 * a : 512 * (a + 1), 512 * b : 512 * (b + 1)].rearrange("(p j) c -> p j c", j=4),
            )

        sc2 = held("sc2", [P, T], U8)
        sc3 = held("sc3", [P, T], U8)
        sc1 = held("sc1", [P, T], U8)
        wsc_raw = held("wsc_raw", [P, H], U8)
        w4sc = held("w4sc", [P, 2 * N], U8)
        nc.gpsimd.memset(sc2[:].bitcast(I32), 0)
        nc.vector.memset(wsc_raw[:].bitcast(I32), 0)
        nc.vector.memset(sc3[:].bitcast(I32), 0)
        nc.vector.memset(sc1[:].bitcast(I32), 0)
        nc.vector.memset(w4sc[:].bitcast(I32), 0)

        warm = held("warm", [P, 1], F32)
        warm2 = held("warm2", [P, 1], F32)
        nc.vector.memset(warm[:], 1.0)
        nc.scalar.activation(warm2[:], warm[:], ACT.Abs_reciprocal_sqrt)

        wb_raw = held("wb_raw", [P, 2 * H], U8)
        l_offs2 = load_list("l_offs2", offs2)
        load_rows(sc2, 0, tab2_scales)
        nc.sync.dma_start(wb_raw[:].bitcast(I32), wb_words[0].bitcast(I32))
        load_rows(wsc_raw, 0, wb_scales, range(1))
        tw2 = load_words("tw2", tab2_words[0])
        load_rows(wsc_raw, 0, wb_scales, range(1, 4))
        load_rows(wsc_raw, 4, wd_scales)
        l_offs3 = load_list("l_offs3", offs3)
        load_rows(sc3, 4, tab3_scales)
        tw3 = load_words("tw3", tab3_words[0])
        wd_raw = load_words("wd_raw", wd_words[0])
        l_offs = load_list("l_offs", offs)
        load_rows(sc1, 8, tab_scales)
        l_pos2 = load_list("l_pos2", pos2)
        load_wa(0, 0)
        load_wa(1, 0)
        tw10 = load_words("tw10", tab_words[0])
        tw11 = load_words("tw11", tab_words[1])
        l_pos3 = load_list("l_pos3", pos3)
        l_pos1 = load_list("l_pos1", pos1)

        def gather(name, window, offsets, dtype):
            t = held(name, [P, 16 * offsets.shape[1]], dtype)
            nc.vector.tensor_copy(t[:], window[:].indirect(offsets))
            return t

        def product(win, h, passes):
            cols = slice(BANK * h, BANK * (h + 1))
            acc = next_bank()
            for i, (w, ws, v, vs) in enumerate(passes):
                nc.tensor.matmul_mx(
                    out=acc[:], lhsT=w, lhsT_scale=ws, rhs=v.bitcast(FP8X4), rhs_scale=vs,
                    start=(i == 0), stop=(i == len(passes) - 1),
                )
            nc.scalar.copy(win[:, cols], acc[:])

        def halves(ap):
            return [ap[:, BANK * h : BANK * (h + 1)] for h in range(2)]

        win_b, win_d, win_a = {}, {}, {}
        picked_b, picked_d, diff, damp = {}, {}, {}, {}
        wa_codes, wa_sc = {}, {}

        wb = held("wb", [P, 2 * H], U8)
        wsc = held("wsc", [P, H], U8)
        gs2, gw2 = [], []
        for h in range(2):
            entries = l_offs2[:, BANK // 16 * h : BANK // 16 * (h + 1)]
            gs2.append(gather("gs2_%d" % h, sc2, entries, U8))
            if h == 0:
                nc.vector.tensor_copy(
                    wb[:].bitcast(U16).rearrange("p (b t q) -> p b t q", b=2, t=4),
                    wb_raw[:].bitcast(U16).rearrange("p (b q t) -> p b t q", b=2, t=4),
                )
                nc.vector.tensor_copy(
                    wsc[:].rearrange("p (b t q) -> p b t q", b=2, t=4),
                    wsc_raw[:].rearrange("p (b q t) -> p b t q", b=2, t=4),
                )
            gw2.append(gather("gw2_%d" % h, tw2, entries, U32))

        def make_b(b):
            for u in range(4 * b, 4 * b + 4):
                win_b[u] = held("win_b%d" % u, [P, S], F32, "win%d" % (u + 4 * b))
            for h in range(2):
                for u in range(4 * b, 4 * b + 4):
                    product(win_b[u], h, [(
                        wb[:, 2 * P * u : 2 * P * (u + 1)].bitcast(FP4X4), wsc[:, P * u : P * (u + 1)],
                        gw2[h][:], gs2[h][:],
                    )])

        make_b(0)
        gs3 = gather("gs3", sc3, l_offs3[:], U8)
        gw3 = gather("gw3", tw3, l_offs3[:], U32)
        wd = held("wd", [P, H], U32)
        for b in range(2):
            cols = slice(BANK * b, BANK * (b + 1))
            nc.vector.tensor_copy(
                wd[:, cols].bitcast(I32).rearrange("p (t g i) -> p g t i", t=4, i=4),
                wd_raw[:, cols].bitcast(I32).rearrange("p (g i t) -> p g t i", t=4, i=4),
            )

        w5_raw = held("w5_raw", [P, 2, 4, N], F32)
        for a in range(2):
            nc.sync.dma_start(w5_raw[:, a], w5[512 * a : 512 * (a + 1), :].rearrange("(p j) c -> p j c", j=4))
        load_wa(0, 1, "tw2")
        load_wa(1, 1, "tw3")
        w4w = held("w4w", [P, 2, 2 * N], U8)
        nc.sync.dma_start(w4w[:].bitcast(I32), w4_words.rearrange("a p c -> p a c").bitcast(I32))
        for q in range(4):
            nc.sync.dma_start(
                w4sc[32 * q : 32 * q + 4, :].rearrange("r (a c) -> r a c", a=2).bitcast(I32),
                w4_scales[:, 4 * q : 4 * q + 4, :].rearrange("a r c -> r a c").bitcast(I32),
            )
        base_sb = held("base_sb", [P, 2], F32)
        with nc.allow_non_contiguous_dma(reason="one value of base a partition"):
            nc.sync.dma_start(base_sb[:], base.rearrange("(c p) -> p c", p=P))

        acc4, acc5, zq = {}, {}, {}
        w5_codes = held("w5_codes", [P, 2 * N], U32)
        w5_sc = held("w5_sc", [P, 2 * N], U8)

        def pick(wins_of, b, entries, into):
            for t in range(4):
                nc.vector.tensor_copy(into[:, t, :], wins_of[4 * b + t][:].indirect(entries[:]))

        def pick_b(b):
            if b == 0:
                picked_b[b] = held("picked_b0", [P, 4, J], F32)
            else:
                picked_b[b] = held("picked_b1", [P, 4, J], F32, "picked_d0")
            pick(win_b, b, l_pos2, picked_b[b])

        def pick_d(b):
            picked_d[b] = held("picked_d%d" % b, [P, 4, J], F32)
            pick(win_d, b, l_pos3, picked_d[b])

        def make_d(b):
            for u in range(4 * b, 4 * b + 4):
                win_d[u] = held("win_d%d" % u, [P, S], F32, "win%d" % ((4 + u) % 8))
                for h in range(2):
                    product(win_d[u], h, [(
                        wd[:, P * u : P * (u + 1)].bitcast(FP8X4), wsc[4:P, P * u : P * (u + 1)],
                        halves(gw3)[h], halves(gs3[4:P, :])[h],
                    )])

        def gpsimd_copy(dst, src):
            nc.gpsimd.tensor_scalar(dst, src, 1.0, 0.0, ALU.mult, ALU.add)

        def quantise_wa(a, b):
            grouped = held("grouped%d%d" % (a, b), [P, BANK * 4], BF16, "grouped%d" % a)
            dst = grouped[:].rearrange("p (t m j) -> p m t j", t=4, j=4)
            src = wa_raw[a, b][:].rearrange("p j (m t) -> p m t j", t=4)
            for m0 in range(0, P, 64):
                gpsimd_copy(dst[:, m0 : m0 + 64], src[:, m0 : m0 + 64])
            wa_codes[a, b] = held("wa_codes%d%d" % (a, b), [P, BANK], U32)
            wa_sc[a, b] = held("wa_sc%d%d" % (a, b), [P, BANK], U8)
            nc.vector.quantize_mx(wa_codes[a, b][:].bitcast(FP8X4), wa_sc[a, b][:], grouped[:])

        def quantise_w5(engine_copy):
            grouped = held("grouped_w5", [P, BANK * 4], BF16)
            for a in range(2):
                engine_copy(
                    grouped[:, 4 * N * a : 4 * N * (a + 1)].rearrange("p (c j) -> p c j", j=4),
                    w5_raw[:, a].rearrange("p j c -> p c j"),
                )
            nc.vector.quantize_mx(w5_codes[:].bitcast(FP8X4), w5_sc[:], grouped[:])

        def make_damp(b):
            damp[b] = held("damp%d" % b, [P, 4, J], F32)
            for half in range(2):
                part = damp[b][:, 2 * half : 2 * half + 2, :]
                nc.scalar.activation(part, picked_b[b][:, 2 * half : 2 * half + 2, :], ACT.Square)
                nc.scalar.activation(part, part, ACT.Abs_reciprocal_sqrt, bias=1.0)
                nc.scalar.activation(part, part, ACT.Square)

        def make_a(b):
            for t in range(4):
                cols = slice(P * t, P * (t + 1))
                win_a[4 * b + t] = held("win_a%d" % (4 * b + t), [P, S], F32, "win%d" % (4 * b + t))
                for h in range(2):
                    product(win_a[4 * b + t], h, [
                        (wa_codes[a, b][:, cols].bitcast(FP8X4), wa_sc[a, b][:, cols],
                         halves(gw1[a])[h], halves(gs1[8 + 4 * a : P, :])[h])
                        for a in range(2)
                    ])

        def pick_a(b):
            diff[b] = held("diff%d" % b, [P, 4, J], F32, ("grouped1", "picked_b0")[b])
            for t in range(4):
                nc.vector.tensor_tensor(
                    diff[b][:, t, :], win_a[4 * b + t][:].indirect(l_pos1[:]), picked_d[b][:, t, :], ALU.subtract
                )

        def second_stage(b, engine, width, run):
            z_codes = ring.tile([P, J], U32, name="z_codes", align_bytes=64)
            z_sc = ring.tile([P, J], U8, name="z_sc", align_bytes=64)
            for j0 in range(0, J, width):
                if j0 % run == 0:
                    z = held("z%d_%d" % (b, j0), [P, run * 4], BF16, "z%d" % b)
                at = j0 % run
                engine.tensor_tensor(
                    z[:, 4 * at : 4 * (at + width)].rearrange("p (c i t) -> p c t i", i=4, t=4),
                    diff[b][:, :, j0 : j0 + width].rearrange("p t (c i) -> p c t i", i=4),
                    damp[b][:, :, j0 : j0 + width].rearrange("p t (c i) -> p c t i", i=4),
                    ALU.mult,
                )
                j1 = j0 + width
                if j1 % run == 0:
                    nc.vector.quantize_mx(
                        z_codes[:, j1 - run : j1].bitcast(FP8X4), z_sc[:, j1 - run : j1], z[:]
                    )
            zq[b] = z_codes, z_sc

        def multiply_z(b):
            z_codes, z_sc = zq[b]
            for h in range(2):
                if b == 0:
                    acc4[h] = next_bank()
                    acc5[h] = next_bank()
                for c in range(2):
                    wcols = slice(N * b + P * c, N * b + P * (c + 1))
                    for y in range(2):
                        zc = slice(HALF * h + P * y, HALF * h + P * (y + 1))
                        nc.tensor.matmul_mx(
                            out=acc4[h][:, HALF * c + P * y : HALF * c + P * (y + 1)],
                            lhsT=w4w[:, b, 2 * P * c : 2 * P * (c + 1)].bitcast(FP4X4),
                            lhsT_scale=w4sc[:, wcols], rhs=z_codes[:, zc].bitcast(FP8X4), rhs_scale=z_sc[:, zc],
                            start=(b == 0 and c == 0 and y == 0), stop=(b == 1 and c == 1 and y == 1),
                        )
                zc = slice(HALF * h, HALF * (h + 1))
                for c in range(2):
                    wcols = slice(N * b + P * c, N * b + P * (c + 1))
                    nc.tensor.matmul_mx(
                        out=acc5[h][:, HALF * c : HALF * (c + 1)], lhsT=w5_codes[:, wcols].bitcast(FP8X4),
                        lhsT_scale=w5_sc[:, wcols], rhs=z_codes[:, zc].bitcast(FP8X4), rhs_scale=z_sc[:, zc],
                        start=(b == 0 and c == 0), stop=(b == 1 and c == 1),
                    )
                if b == 1:
                    size = ring.tile([P, BANK], F32, name="size")
                    res = ring.tile([P, 2, HALF], F32, name="res")
                    for c in range(2):
                        cols = slice(HALF * c, HALF * (c + 1))
                        nc.scalar.activation(size[:, cols], acc4[h][:, cols], ACT.Abs)
                        nc.vector.scalar_tensor_tensor(
                            res[:, c, :], acc5[h][:, cols], base_sb[:, c : c + 1], size[:, cols], ALU.add, ALU.add
                        )
                        nc.sync.dma_start(out[P * c : P * (c + 1), HALF * h : HALF * (h + 1)], res[:, c, :])

        pick_b(0)
        make_d(0)
        quantise_wa(0, 0)
        quantise_wa(1, 0)
        gs1 = gather("gs1", sc1, l_offs[:], U8)
        gw1 = [gather("gw10", tw10, l_offs[:], U32), gather("gw11", tw11, l_offs[:], U32)]
        make_damp(0)
        quantise_w5(gpsimd_copy)
        quantise_wa(0, 1)
        quantise_wa(1, 1)
        make_b(1)
        make_a(0)
        pick_d(0)
        pick_a(0)
        pick_b(1)
        make_d(1)
        second_stage(0, nc.gpsimd, 64, J)
        pick_d(1)
        make_a(1)
        multiply_z(0)
        make_damp(1)
        pick_a(1)
        second_stage(1, nc.vector, 256, 256)
        multiply_z(1)
